import numpy as np, ml_dtypes
CORES = [21,109,149,237,277,365,405,493,150,406]
N = 10
WB, KB, QP = 3, 1, 512
def setup_inputs(rng):
    return {"q": rng.standard_normal((N, 128, QP), dtype=np.float32).astype(ml_dtypes.bfloat16), "k": rng.standard_normal((N, 128, KB * 128), dtype=np.float32).astype(ml_dtypes.bfloat16), "v": rng.standard_normal((N, 128, KB * 128), dtype=np.float32).astype(ml_dtypes.bfloat16)}
def setup_inputs_big(rng):
    d = setup_inputs(rng)
    for k in ("q", "k", "v"): d[k] = (d[k].astype(np.float32) * 1024.0).astype(d[k].dtype)
    return d
def setup_inputs_small(rng):
    d = setup_inputs(rng)
    for k in ("q", "k", "v"): d[k] = (d[k].astype(np.float32) * (1 / 1024.0)).astype(d[k].dtype)
    return d
def setup_inputs_apart(rng):
    d = setup_inputs(rng)
    f = (10.0 ** rng.permutation(np.linspace(-1.5, 1.5, N))).astype(np.float32).reshape(N, 1, 1)
    for k in ("q", "k", "v"): d[k] = (d[k].astype(np.float32) * f).astype(d[k].dtype)
    return d
def reference(q, k, v):
    Q, K, V = q.astype(np.float64), k.astype(np.float64), v.astype(np.float64)
    y = np.zeros((N, 128, QP))
    for r in range(N):
        for j in range(max(0, r - WB), r + 1):
            for b in range(KB):
                S = np.maximum(K[j][:, 128 * b:128 * b + 128].T @ Q[r], 0.0)
                y[r] += V[j][:, 128 * b:128 * b + 128].T @ S
    return {"y": y.astype(ml_dtypes.bfloat16 if q.dtype != np.float64 else np.float64)}

@@ -1,0 +1,233 @@
+from concourse.bass import DstId, RemoteDMATransfer
+from concourse.mybir import AluOpType
+
+WORLD = 512
+P, KW, QP, WB = 128, 128, 512, 3
+KV = 2 * KW
+HALF = QP // 2
+N_RELAY = 4
+N_LAND = 8
+
+SCRATCH = {
+    "kvd": ("dram", [P, KV], "bfloat16"),
+    "rly": ("dram", [P, KV], "bfloat16"),
+    "kvo": ("sbuf", [P, KV], "bfloat16"),
+    "kin": ("sbuf", [P, WB * KV], "bfloat16"),
+    "qs": ("sbuf", [P, QP], "bfloat16"),
+    "zero": ("sbuf", [P, QP], "float32"),
+    "ys": ("sbuf", [P, QP], "bfloat16"),
+}
+for _i in range(WB + 1):
+    SCRATCH["s%d" % _i] = ("sbuf", [P, QP], "bfloat16")
+for _i in range(6):
+    SCRATCH["pS%d" % _i] = ("psum", [P, QP], "float32")
+for _i in range(2):
+    SCRATCH["pO%d" % _i] = ("psum", [P, QP], "float32")
+
+SEMAPHORES = ["ldk", "ldo", "zf", "rl", "snt", "arr1", "arr2", "arr3", "om0", "om1", "cp0", "cp1", "st"]
+for _i in range(WB + 1):
+    SEMAPHORES += ["sm%d0" % _i, "sm%d1" % _i, "rr%d0" % _i, "rr%d1" % _i]
+
+_CACHE = {}
+
+
+def _bits(mask):
+    return [b for b in range(16) if (mask >> b) & 1]
+
+
+def _mask(bits):
+    return sum(1 << b for b in bits)
+
+
+def _spread(bits, n, k=0):
+    if 2 * n * (k + 1) <= len(bits):
+        return bits[2 * n * k:2 * n * (k + 1):2]
+    return bits[n * k:n * (k + 1)]
+
+
+def _plan(cores, topo):
+    if "flows" in _CACHE:
+        return _CACHE["flows"]
+    n = len(cores)
+    world = range(WORLD)
+    ranks = set(cores)
+    used = set()
+
+    def same_chip(a, b):
+        return topo.host(a) == topo.host(b) and topo.chip(a) == topo.chip(b)
+
+    flows = []
+    for j, s in enumerate(cores):
+        mine = []
+        for r in range(j + 1, min(j + WB, n - 1) + 1):
+            t = cores[r]
+            f = {"j": j, "r": r, "src": s, "dst": t, "via": None, "cls": 1, "m1": 0, "m2": 0}
+            mine.append(f)
+            if topo.may_write(s, t):
+                continue
+            near = [x for x in world if same_chip(x, s) and x not in ranks and x not in used
+                    and topo.may_write(s, x) and topo.may_write(x, t)]
+            if near:
+                own = r - j == 1 and topo.rack(topo.host(s)) == topo.rack(topo.host(t))
+                near.sort(key=lambda x: ((topo.die(x) == topo.die(s)) != own, x))
+                f["via"], f["cls"] = near[0], 3
+            else:
+                far = []
+                for x in world:
+                    if x in used or not topo.same_plane(s, x) or not topo.may_write(s, x) or not topo.may_write(x, t):
+                        continue
+                    if topo.chip(x) == topo.chip(t):
+                        far.append((0, x not in ranks, topo.die(x) != topo.die(s), x))
+                    elif any(topo.mates(x, y) and topo.chip(y) == topo.chip(t)
+                             for y in world if topo.host(y) == topo.host(x)):
+                        far.append((1, x in ranks, topo.die(x) != topo.die(s), x))
+                far.sort()
+                f["via"] = far[0][-1]
+                f["cls"] = 2 if f["via"] in ranks else 4
+            used.add(f["via"])
+        k_on = 0
+        taken = 0
+        for f in mine:
+            x = f["via"]
+            if x is None:
+                f["m2"] = _mask(_bits(topo.mask(s, f["dst"]))[:N_LAND])
+                continue
+            if same_chip(s, x):
+                m = _mask(_spread(_bits(topo.mask(s, x))[::-1], N_RELAY, k_on))
+                k_on += 1
+            else:
+                m = _mask(_spread(_bits(topo.mask(s, x)), N_RELAY))
+            assert m and not (m & taken)
+            taken |= m
+            f["m1"] = m
+            f["m2"] = _mask(_bits(topo.mask(x, f["dst"]))[:N_LAND])
+        flows += mine
+    _CACHE["flows"] = flows
+    return flows
+
+
+def _count(mask):
+    return len(_bits(mask))
+
+
+def rank_program(g, core, T, topo):
+    flows = _plan(T.cores, topo)
+    rank = T.rank_of(core)
+    sem = T.sem
+    out = [f for f in flows if f["src"] == core]
+    thru = [f for f in flows if f["via"] == core]
+    if rank is None and not thru:
+        return
+
+    if rank is not None:
+        if out:
+            g.sync.dma_start(T.kvd[:, 0:KW], T.k[:, :]).then_inc(sem.ldk, 16)
+            g.scalar.dma_start(T.kvd[:, KW:KV], T.v[:, :]).then_inc(sem.ldk, 16)
+        g.sync.dma_start(T.qs[:, :], T.q[:, :]).then_inc(sem.ldo, 16)
+        g.scalar.dma_start(T.kvo[:, 0:KW], T.k[:, :]).then_inc(sem.ldo, 16)
+        g.scalar.dma_start(T.kvo[:, KW:KV], T.v[:, :]).then_inc(sem.ldo, 16)
+
+    sent = 0
+
+    def land(f):
+        d = f["r"] - f["j"]
+        return T.kin[:, (d - 1) * KV:d * KV], sem["arr%d" % d]
+
+    if out:
+        g.wait_ge(sem.ldk, 32)
+        hop1 = []
+        for f in out:
+            if f["via"] is not None:
+                rid, pid = topo.addr(f["via"], core)
+                hop1.append(RemoteDMATransfer(dst_ids=[DstId(rid=rid, pnc=pid)], dma_engine_mask=f["m1"],
+                                              remote_sem=sem.rl, src=T.kvd[:], dst=T.rly[:]))
+                sent += _count(f["m1"])
+        if hop1:
+            g.remote_dma_fused(hop1, local_sem=sem.snt)
+        for f in out:
+            if f["via"] is None:
+                rid, pid = topo.addr(f["dst"], core)
+                dst, arr = land(f)
+                g.remote_dma(out_ap=dst, in_ap=T.kvd[:], remote_sem=arr, local_sem=sem.snt, pid=pid, routing_id=rid,
+                             dma_engine_mask=f["m2"])
+                sent += _count(f["m2"])
+    for f in thru:
+        g.wait_ge(sem.rl, _count(f["m1"]))
+        rid, pid = topo.addr(f["dst"], core)
+        dst, arr = land(f)
+        g.remote_dma(out_ap=dst, in_ap=T.rly[:], remote_sem=arr, local_sem=sem.snt, pid=pid, routing_id=rid,
+                     dma_engine_mask=f["m2"])
+        sent += _count(f["m2"])
+    if sent:
+        g.wait_ge(sem.snt, sent)
+    if rank is None:
+        return
+
+    blocks = [None] + sorted([f for f in flows if f["dst"] == core], key=lambda f: (f["cls"], f["j"]))
+    nb = len(blocks)
+    te, ve = g.tensor, g.vector
+    split = [i >= nb - 2 for i in range(nb)]
+    bank = []
+    b = 0
+    for i in range(nb):
+        bank.append(b)
+        b += 2 if split[i] else 1
+
+    def kv(i):
+        f = blocks[i]
+        if f is None:
+            return T.kvo[:, 0:KW], T.kvo[:, KW:KV]
+        c = (f["r"] - f["j"] - 1) * KV
+        return T.kin[:, c:c + KW], T.kin[:, c + KW:c + KV]
+
+    ve.memset(T.zero[:, :], 0.0).then_inc(sem.zf, 1)
+    ve.wait_ge(sem.zf, 1)
+
+    def scores(i):
+        f = blocks[i]
+        if f is None:
+            te.wait_ge(sem.ldo, 48)
+        else:
+            te.wait_ge(sem["arr%d" % (f["r"] - f["j"])], _count(f["m2"]))
+        k_ap = kv(i)[0]
+        s_sb = T["s%d" % i]
+        if split[i]:
+            for h in range(2):
+                ps = T["pS%d" % (bank[i] + h)]
+                te.matmul(ps[:, 0:HALF], k_ap, T.qs[:, h * HALF:(h + 1) * HALF], True, True).then_inc(sem["sm%d%d" % (i, h)], 1)
+                ve.wait_ge(sem["sm%d%d" % (i, h)], 1)
+                ve.tensor_tensor(s_sb[:, h * HALF:(h + 1) * HALF], ps[:, 0:HALF], T.zero[:, 0:HALF],
+                                 AluOpType.max).then_inc(sem["rr%d%d" % (i, h)], 1)
+        else:
+            ps = T["pS%d" % bank[i]]
+            te.matmul(ps[:, :], k_ap, T.qs[:, :], True, True).then_inc(sem["sm%d0" % i], 1)
+            ve.wait_ge(sem["sm%d0" % i], 1)
+            ve.tensor_tensor(s_sb[:, :], ps[:, :], T.zero[:, :], AluOpType.max).then_inc(sem["rr%d0" % i], 1)
+
+    def values(i):
+        v_ap = kv(i)[1]
+        s_sb = T["s%d" % i]
+        for h in range(2):
+            if split[i] or h == 0:
+                te.wait_ge(sem["rr%d%d" % (i, h)], 1)
+            mm = te.matmul(T["pO%d" % h][:, 0:HALF], v_ap, s_sb[:, h * HALF:(h + 1) * HALF], i == 0, i == nb - 1)
+            if i == nb - 1:
+                mm.then_inc(sem["om%d" % h], 1)
+
+    pending = None
+    for i in range(nb):
+        scores(i)
+        if pending is not None:
+            values(pending)
+            pending = None
+        if i + 1 < nb and blocks[i] is not None and blocks[i]["cls"] >= 3 and blocks[i + 1]["cls"] >= 3:
+            pending = i
+        else:
+            values(i)
+
+    for h, q in ((0, g.sync), (1, g.scalar)):
+        ve.wait_ge(sem["om%d" % h], 1)
+        ve.tensor_copy(T.ys[:, h * HALF:(h + 1) * HALF], T["pO%d" % h][:, 0:HALF]).then_inc(sem["cp%d" % h], 1)
+        q.wait_ge(sem["cp%d" % h], 1)
+        q.dma_start(T.y[:, h * HALF:(h + 1) * HALF], T.ys[:, h * HALF:(h + 1) * HALF]).then_inc(sem.st, 16)
+    g.sync.wait_ge(sem.st, 32)

@@ -5,12 +5,14 @@ WORLD = 512
 P, KW, QP, WB = 128, 128, 512, 3
 KV = 2 * KW
 HALF = QP // 2
-N_RELAY = 4
+N_RELAY = 2
 N_LAND = 8
 
 SCRATCH = {
-    "kvd": ("dram", [P, KV], "bfloat16"),
-    "rly": ("dram", [P, KV], "bfloat16"),
+    "kv0": ("dram", [P, KW], "bfloat16"),
+    "kv1": ("dram", [P, KW], "bfloat16"),
+    "rl0": ("dram", [P, KW], "bfloat16"),
+    "rl1": ("dram", [P, KW], "bfloat16"),
     "kvo": ("sbuf", [P, KV], "bfloat16"),
     "kin": ("sbuf", [P, WB * KV], "bfloat16"),
     "qs": ("sbuf", [P, QP], "bfloat16"),
@@ -24,7 +26,7 @@ for _i in range(6):
 for _i in range(2):
     SCRATCH["pO%d" % _i] = ("psum", [P, QP], "float32")
 
-SEMAPHORES = ["ldk", "ldo", "zf", "rl", "snt", "arr1", "arr2", "arr3", "om0", "om1", "cp0", "cp1", "st"]
+SEMAPHORES = ["ldk", "ldo", "zf", "rl", "snt", "a01", "a02", "a03", "a11", "a12", "a13", "om0", "om1", "cp0", "cp1", "st"]
 for _i in range(WB + 1):
     SEMAPHORES += ["sm%d0" % _i, "sm%d1" % _i, "rr%d0" % _i, "rr%d1" % _i]
 
@@ -37,6 +39,10 @@ def _bits(mask):
 
 def _mask(bits):
     return sum(1 << b for b in bits)
+
+
+def _count(mask):
+    return len(_bits(mask))
 
 
 def _spread(bits, n, k=0):
@@ -61,20 +67,20 @@ def _plan(cores, topo):
         mine = []
         for r in range(j + 1, min(j + WB, n - 1) + 1):
             t = cores[r]
-            f = {"j": j, "r": r, "src": s, "dst": t, "via": None, "cls": 1, "m1": 0, "m2": 0}
+            f = {"j": j, "r": r, "src": s, "dst": t, "cls": 1, "legs": [{"via": None}, {"via": None}]}
             mine.append(f)
             if topo.may_write(s, t):
                 continue
-            near = [x for x in world if same_chip(x, s) and x not in ranks and x not in used
-                    and topo.may_write(s, x) and topo.may_write(x, t)]
+            ok = [x for x in world if x != s and x != t and x not in used and topo.may_write(s, x) and topo.may_write(x, t)]
+            near = [x for x in ok if same_chip(x, s)]
             if near:
                 own = r - j == 1 and topo.rack(topo.host(s)) == topo.rack(topo.host(t))
-                near.sort(key=lambda x: ((topo.die(x) == topo.die(s)) != own, x))
-                f["via"], f["cls"] = near[0], 3
+                near.sort(key=lambda x: ((topo.die(x) == topo.die(s)) != own, x in ranks, x))
+                via, f["cls"] = near[:2], 3
             else:
                 far = []
-                for x in world:
-                    if x in used or not topo.same_plane(s, x) or not topo.may_write(s, x) or not topo.may_write(x, t):
+                for x in ok:
+                    if not topo.same_plane(s, x):
                         continue
                     if topo.chip(x) == topo.chip(t):
                         far.append((0, x not in ranks, topo.die(x) != topo.die(s), x))
@@ -82,32 +88,34 @@ def _plan(cores, topo):
                              for y in world if topo.host(y) == topo.host(x)):
                         far.append((1, x in ranks, topo.die(x) != topo.die(s), x))
                 far.sort()
-                f["via"] = far[0][-1]
-                f["cls"] = 2 if f["via"] in ranks else 4
-            used.add(f["via"])
-        k_on = 0
-        taken = 0
+                if far[0][-1] in ranks:
+                    via, f["cls"] = [far[0][-1]] * 2, 2
+                else:
+                    via, f["cls"] = [far[0][-1], far[1][-1]], 4
+            for leg, x in zip(f["legs"], via):
+                leg["via"] = x
+                used.add(x)
+        k_on = k_off = taken = 0
         for f in mine:
-            x = f["via"]
-            if x is None:
-                f["m2"] = _mask(_bits(topo.mask(s, f["dst"]))[:N_LAND])
-                continue
-            if same_chip(s, x):
-                m = _mask(_spread(_bits(topo.mask(s, x))[::-1], N_RELAY, k_on))
-                k_on += 1
-            else:
-                m = _mask(_spread(_bits(topo.mask(s, x)), N_RELAY))
-            assert m and not (m & taken)
-            taken |= m
-            f["m1"] = m
-            f["m2"] = _mask(_bits(topo.mask(x, f["dst"]))[:N_LAND])
+            one = f["legs"][0]["via"] == f["legs"][1]["via"]
+            for i, leg in enumerate(f["legs"]):
+                x = leg["via"]
+                last = _bits(topo.mask(s if x is None else x, f["dst"]))[:N_LAND]
+                leg["m2"] = _mask(last[i * len(last) // 2:(i + 1) * len(last) // 2] if one else last)
+                leg["m1"] = 0
+                if x is None:
+                    continue
+                if same_chip(s, x):
+                    leg["m1"] = _mask(_spread(_bits(topo.mask(s, x))[::-1], N_RELAY, k_on))
+                    k_on += 1
+                else:
+                    leg["m1"] = _mask(_spread(_bits(topo.mask(s, x)), N_RELAY, k_off))
+                    k_off += 1
+                assert leg["m1"] and not (leg["m1"] & taken)
+                taken |= leg["m1"]
         flows += mine
     _CACHE["flows"] = flows
     return flows
-
-
-def _count(mask):
-    return len(_bits(mask))
 
 
 def rank_program(g, core, T, topo):
@@ -115,51 +123,46 @@ def rank_program(g, core, T, topo):
     rank = T.rank_of(core)
     sem = T.sem
     out = [f for f in flows if f["src"] == core]
-    thru = [f for f in flows if f["via"] == core]
+    thru = [f for f in flows if core in (f["legs"][0]["via"], f["legs"][1]["via"])]
     if rank is None and not thru:
         return
 
     if rank is not None:
         if out:
-            g.sync.dma_start(T.kvd[:, 0:KW], T.k[:, :]).then_inc(sem.ldk, 16)
-            g.scalar.dma_start(T.kvd[:, KW:KV], T.v[:, :]).then_inc(sem.ldk, 16)
+            g.sync.dma_start(T.kv0[:, :], T.k[:, :]).then_inc(sem.ldk, 16)
+            g.scalar.dma_start(T.kv1[:, :], T.v[:, :]).then_inc(sem.ldk, 16)
         g.sync.dma_start(T.qs[:, :], T.q[:, :]).then_inc(sem.ldo, 16)
         g.scalar.dma_start(T.kvo[:, 0:KW], T.k[:, :]).then_inc(sem.ldo, 16)
         g.scalar.dma_start(T.kvo[:, KW:KV], T.v[:, :]).then_inc(sem.ldo, 16)
 
-    sent = 0
+    sent = [0]
 
-    def land(f):
+    def xfer(dst_core, mask, remote_sem, src, dst):
+        rid, pid = topo.addr(dst_core, core)
+        sent[0] += _count(mask)
+        return RemoteDMATransfer(dst_ids=[DstId(rid=rid, pnc=pid)], dma_engine_mask=mask, remote_sem=remote_sem,
+                                 src=src, dst=dst)
+
+    def land(f, i, src):
         d = f["r"] - f["j"]
-        return T.kin[:, (d - 1) * KV:d * KV], sem["arr%d" % d]
+        c = (d - 1) * KV + i * KW
+        return xfer(f["dst"], f["legs"][i]["m2"], sem["a%d%d" % (i, d)], src, T.kin[:, c:c + KW])
 
     if out:
         g.wait_ge(sem.ldk, 32)
-        hop1 = []
-        for f in out:
-            if f["via"] is not None:
-                rid, pid = topo.addr(f["via"], core)
-                hop1.append(RemoteDMATransfer(dst_ids=[DstId(rid=rid, pnc=pid)], dma_engine_mask=f["m1"],
-                                              remote_sem=sem.rl, src=T.kvd[:], dst=T.rly[:]))
-                sent += _count(f["m1"])
+        hop1 = [xfer(leg["via"], leg["m1"], sem.rl, T["kv%d" % i][:], T["rl%d" % i][:])
+                for f in out for i, leg in enumerate(f["legs"]) if leg["via"] is not None]
         if hop1:
             g.remote_dma_fused(hop1, local_sem=sem.snt)
         for f in out:
-            if f["via"] is None:
-                rid, pid = topo.addr(f["dst"], core)
-                dst, arr = land(f)
-                g.remote_dma(out_ap=dst, in_ap=T.kvd[:], remote_sem=arr, local_sem=sem.snt, pid=pid, routing_id=rid,
-                             dma_engine_mask=f["m2"])
-                sent += _count(f["m2"])
+            if f["legs"][0]["via"] is None:
+                g.remote_dma_fused([land(f, i, T["kv%d" % i][:]) for i in range(2)], local_sem=sem.snt)
     for f in thru:
-        g.wait_ge(sem.rl, _count(f["m1"]))
-        rid, pid = topo.addr(f["dst"], core)
-        dst, arr = land(f)
-        g.remote_dma(out_ap=dst, in_ap=T.rly[:], remote_sem=arr, local_sem=sem.snt, pid=pid, routing_id=rid,
-                     dma_engine_mask=f["m2"])
-        sent += _count(f["m2"])
-    if sent:
-        g.wait_ge(sem.snt, sent)
+        mine = [i for i in range(2) if f["legs"][i]["via"] == core]
+        g.wait_ge(sem.rl, sum(_count(f["legs"][i]["m1"]) for i in mine))
+        g.remote_dma_fused([land(f, i, T["rl%d" % i][:]) for i in mine], local_sem=sem.snt)
+    if sent[0]:
+        g.wait_ge(sem.snt, sent[0])
     if rank is None:
         return
 
@@ -188,7 +191,7 @@ def rank_program(g, core, T, topo):
         if f is None:
             te.wait_ge(sem.ldo, 48)
         else:
-            te.wait_ge(sem["arr%d" % (f["r"] - f["j"])], _count(f["m2"]))
+            te.wait_ge(sem["a0%d" % (f["r"] - f["j"])], _count(f["legs"][0]["m2"]))
         k_ap = kv(i)[0]
         s_sb = T["s%d" % i]
         if split[i]:
@@ -207,6 +210,9 @@ def rank_program(g, core, T, topo):
     def values(i):
         v_ap = kv(i)[1]
         s_sb = T["s%d" % i]
+        f = blocks[i]
+        if f is not None:
+            te.wait_ge(sem["a1%d" % (f["r"] - f["j"])], _count(f["legs"][1]["m2"]))
         for h in range(2):
             if split[i] or h == 0:
                 te.wait_ge(sem["rr%d%d" % (i, h)], 1)

from concourse.bass import DstId, RemoteDMATransfer
from concourse.mybir import AluOpType

WORLD = 512
P, KW, QP, WB = 128, 128, 512, 3
KV = 2 * KW
HALF = QP // 2
N_RELAY = 2
N_LAND = 8

SCRATCH = {
    "kv0": ("dram", [P, KW], "bfloat16"),
    "kv1": ("dram", [P, KW], "bfloat16"),
    "rl0": ("dram", [P, KW], "bfloat16"),
    "rl1": ("dram", [P, KW], "bfloat16"),
    "kvo": ("sbuf", [P, KV], "bfloat16"),
    "kin": ("sbuf", [P, WB * KV], "bfloat16"),
    "qs": ("sbuf", [P, QP], "bfloat16"),
    "zero": ("sbuf", [P, QP], "float32"),
    "ys": ("sbuf", [P, QP], "bfloat16"),
}
for _i in range(WB + 1):
    SCRATCH["s%d" % _i] = ("sbuf", [P, QP], "bfloat16")
for _i in range(6):
    SCRATCH["pS%d" % _i] = ("psum", [P, QP], "float32")
for _i in range(2):
    SCRATCH["pO%d" % _i] = ("psum", [P, QP], "float32")

SEMAPHORES = ["ldk", "ldo", "zf", "rl", "snt", "a01", "a02", "a03", "a11", "a12", "a13", "om0", "om1", "cp0", "cp1", "st"]
for _i in range(WB + 1):
    SEMAPHORES += ["sm%d0" % _i, "sm%d1" % _i, "rr%d0" % _i, "rr%d1" % _i]

_CACHE = {}


def _bits(mask):
    return [b for b in range(16) if (mask >> b) & 1]


def _mask(bits):
    return sum(1 << b for b in bits)


def _count(mask):
    return len(_bits(mask))


def _spread(bits, n, k=0):
    if 2 * n * (k + 1) <= len(bits):
        return bits[2 * n * k:2 * n * (k + 1):2]
    return bits[n * k:n * (k + 1)]


def _plan(cores, topo):
    if "flows" in _CACHE:
        return _CACHE["flows"]
    n = len(cores)
    world = range(WORLD)
    ranks = set(cores)
    used = set()

    def same_chip(a, b):
        return topo.host(a) == topo.host(b) and topo.chip(a) == topo.chip(b)

    flows = []
    for j, s in enumerate(cores):
        mine = []
        for r in range(j + 1, min(j + WB, n - 1) + 1):
            t = cores[r]
            f = {"j": j, "r": r, "src": s, "dst": t, "cls": 1, "legs": [{"via": None}, {"via": None}]}
            mine.append(f)
            if topo.may_write(s, t):
                continue
            ok = [x for x in world if x != s and x != t and x not in used and topo.may_write(s, x) and topo.may_write(x, t)]
            near = [x for x in ok if same_chip(x, s)]
            if near:
                own = r - j == 1 and topo.rack(topo.host(s)) == topo.rack(topo.host(t))
                near.sort(key=lambda x: ((topo.die(x) == topo.die(s)) != own, x in ranks, x))
                via, f["cls"] = near[:2], 3
            else:
                far = []
                for x in ok:
                    if not topo.same_plane(s, x):
                        continue
                    if topo.chip(x) == topo.chip(t):
                        far.append((0, x not in ranks, topo.die(x) != topo.die(s), x))
                    elif any(topo.mates(x, y) and topo.chip(y) == topo.chip(t)
                             for y in world if topo.host(y) == topo.host(x)):
                        far.append((1, x in ranks, topo.die(x) != topo.die(s), x))
                far.sort()
                if far[0][-1] in ranks:
                    via, f["cls"] = [far[0][-1]] * 2, 2
                else:
                    via, f["cls"] = [far[0][-1], far[1][-1]], 4
            for leg, x in zip(f["legs"], via):
                leg["via"] = x
                used.add(x)
        k_on = k_off = taken = 0
        for f in mine:
            one = f["legs"][0]["via"] == f["legs"][1]["via"]
            for i, leg in enumerate(f["legs"]):
                x = leg["via"]
                last = _bits(topo.mask(s if x is None else x, f["dst"]))[:N_LAND]
                leg["m2"] = _mask(last[i * len(last) // 2:(i + 1) * len(last) // 2] if one else last)
                leg["m1"] = 0
                if x is None:
                    continue
                if same_chip(s, x):
                    leg["m1"] = _mask(_spread(_bits(topo.mask(s, x))[::-1], N_RELAY, k_on))
                    k_on += 1
                else:
                    leg["m1"] = _mask(_spread(_bits(topo.mask(s, x)), N_RELAY, k_off))
                    k_off += 1
                assert leg["m1"] and not (leg["m1"] & taken)
                taken |= leg["m1"]
        flows += mine
    _CACHE["flows"] = flows
    return flows


def rank_program(g, core, T, topo):
    flows = _plan(T.cores, topo)
    rank = T.rank_of(core)
    sem = T.sem
    out = [f for f in flows if f["src"] == core]
    thru = [f for f in flows if core in (f["legs"][0]["via"], f["legs"][1]["via"])]
    if rank is None and not thru:
        return

    if rank is not None:
        if out:
            g.sync.dma_start(T.kv0[:, :], T.k[:, :]).then_inc(sem.ldk, 16)
            g.scalar.dma_start(T.kv1[:, :], T.v[:, :]).then_inc(sem.ldk, 16)
        g.sync.dma_start(T.qs[:, :], T.q[:, :]).then_inc(sem.ldo, 16)
        g.scalar.dma_start(T.kvo[:, 0:KW], T.k[:, :]).then_inc(sem.ldo, 16)
        g.scalar.dma_start(T.kvo[:, KW:KV], T.v[:, :]).then_inc(sem.ldo, 16)

    sent = [0]

    def xfer(dst_core, mask, remote_sem, src, dst):
        rid, pid = topo.addr(dst_core, core)
        sent[0] += _count(mask)
        return RemoteDMATransfer(dst_ids=[DstId(rid=rid, pnc=pid)], dma_engine_mask=mask, remote_sem=remote_sem,
                                 src=src, dst=dst)

    def land(f, i, src):
        d = f["r"] - f["j"]
        c = (d - 1) * KV + i * KW
        return xfer(f["dst"], f["legs"][i]["m2"], sem["a%d%d" % (i, d)], src, T.kin[:, c:c + KW])

    if out:
        g.wait_ge(sem.ldk, 32)
        hop1 = [xfer(leg["via"], leg["m1"], sem.rl, T["kv%d" % i][:], T["rl%d" % i][:])
                for f in out for i, leg in enumerate(f["legs"]) if leg["via"] is not None]
        if hop1:
            g.remote_dma_fused(hop1, local_sem=sem.snt)
        for f in out:
            if f["legs"][0]["via"] is None:
                g.remote_dma_fused([land(f, i, T["kv%d" % i][:]) for i in range(2)], local_sem=sem.snt)
    for f in thru:
        mine = [i for i in range(2) if f["legs"][i]["via"] == core]
        g.wait_ge(sem.rl, sum(_count(f["legs"][i]["m1"]) for i in mine))
        g.remote_dma_fused([land(f, i, T["rl%d" % i][:]) for i in mine], local_sem=sem.snt)
    if sent[0]:
        g.wait_ge(sem.snt, sent[0])
    if rank is None:
        return

    blocks = [None] + sorted([f for f in flows if f["dst"] == core], key=lambda f: (f["cls"], f["j"]))
    nb = len(blocks)
    te, ve = g.tensor, g.vector
    split = [i >= nb - 2 for i in range(nb)]
    bank = []
    b = 0
    for i in range(nb):
        bank.append(b)
        b += 2 if split[i] else 1

    def kv(i):
        f = blocks[i]
        if f is None:
            return T.kvo[:, 0:KW], T.kvo[:, KW:KV]
        c = (f["r"] - f["j"] - 1) * KV
        return T.kin[:, c:c + KW], T.kin[:, c + KW:c + KV]

    ve.memset(T.zero[:, :], 0.0).then_inc(sem.zf, 1)
    ve.wait_ge(sem.zf, 1)

    def scores(i):
        f = blocks[i]
        if f is None:
            te.wait_ge(sem.ldo, 48)
        else:
            te.wait_ge(sem["a0%d" % (f["r"] - f["j"])], _count(f["legs"][0]["m2"]))
        k_ap = kv(i)[0]
        s_sb = T["s%d" % i]
        if split[i]:
            for h in range(2):
                ps = T["pS%d" % (bank[i] + h)]
                te.matmul(ps[:, 0:HALF], k_ap, T.qs[:, h * HALF:(h + 1) * HALF], True, True).then_inc(sem["sm%d%d" % (i, h)], 1)
                ve.wait_ge(sem["sm%d%d" % (i, h)], 1)
                ve.tensor_tensor(s_sb[:, h * HALF:(h + 1) * HALF], ps[:, 0:HALF], T.zero[:, 0:HALF],
                                 AluOpType.max).then_inc(sem["rr%d%d" % (i, h)], 1)
        else:
            ps = T["pS%d" % bank[i]]
            te.matmul(ps[:, :], k_ap, T.qs[:, :], True, True).then_inc(sem["sm%d0" % i], 1)
            ve.wait_ge(sem["sm%d0" % i], 1)
            ve.tensor_tensor(s_sb[:, :], ps[:, :], T.zero[:, :], AluOpType.max).then_inc(sem["rr%d0" % i], 1)

    def values(i):
        v_ap = kv(i)[1]
        s_sb = T["s%d" % i]
        f = blocks[i]
        if f is not None:
            te.wait_ge(sem["a1%d" % (f["r"] - f["j"])], _count(f["legs"][1]["m2"]))
        for h in range(2):
            if split[i] or h == 0:
                te.wait_ge(sem["rr%d%d" % (i, h)], 1)
            mm = te.matmul(T["pO%d" % h][:, 0:HALF], v_ap, s_sb[:, h * HALF:(h + 1) * HALF], i == 0, i == nb - 1)
            if i == nb - 1:
                mm.then_inc(sem["om%d" % h], 1)

    pending = None
    for i in range(nb):
        scores(i)
        if pending is not None:
            values(pending)
            pending = None
        if i + 1 < nb and blocks[i] is not None and blocks[i]["cls"] >= 3 and blocks[i + 1]["cls"] >= 3:
            pending = i
        else:
            values(i)

    for h, q in ((0, g.sync), (1, g.scalar)):
        ve.wait_ge(sem["om%d" % h], 1)
        ve.tensor_copy(T.ys[:, h * HALF:(h + 1) * HALF], T["pO%d" % h][:, 0:HALF]).then_inc(sem["cp%d" % h], 1)
        q.wait_ge(sem["cp%d" % h], 1)
        q.dma_start(T.y[:, h * HALF:(h + 1) * HALF], T.ys[:, h * HALF:(h + 1) * HALF]).then_inc(sem.st, 16)
    g.sync.wait_ge(sem.st, 32)
